import numpy as np
import ml_dtypes


def mxq(x, axis, fmt="e4m3"):
    dtype, down = {"e4m3": (ml_dtypes.float8_e4m3fn, 7), "e5m2": (ml_dtypes.float8_e5m2, 14)}[fmt]
    v = np.moveaxis(np.asarray(x, np.float32).astype(ml_dtypes.bfloat16).astype(np.float64), axis, -1)
    blocks = v.reshape(v.shape[:-1] + (-1, 32))
    amax = np.abs(blocks).max(-1, keepdims=True)
    byte = np.maximum(np.where(amax > 0, np.frexp(amax)[1] - 1 + 127, 0) - down, 1)
    scale = np.exp2(byte - 127.0)
    codes = (blocks / scale).astype(np.float32).astype(dtype).astype(np.float64)
    return np.moveaxis((codes * scale).reshape(v.shape), -1, axis)


WIDE = False


def mx_kscale(k):
    if not WIDE:
        return np.ones(k)
    levels = np.array([10, -10, 5, -5, 0])
    if k % 512:
        return np.exp2(np.random.permutation(np.resize(levels, k // 32))).repeat(32)
    a = np.empty((k // 512, 16))
    for p in range(k // 512):
        a[p, :8] = np.random.permutation(np.resize(levels, 8))
        for g in range(8):
            far = levels[np.abs(levels - a[p, g]) >= 10]
            a[p, g + 8] = far[np.random.randint(len(far))]
    return np.exp2(a.ravel()).repeat(32)


def f64(x):
    return np.asarray(x).astype(np.float64)


def striped(idx):
    return np.tile(idx.reshape(-1, 16).T, (8, 1)).astype(np.uint16)


def unstriped(offs):
    return offs[:16].T.reshape(-1).astype(np.int64)


def pack_weight(w):
    k, n = w.shape
    w = f64(np.asarray(w, np.float32).astype(ml_dtypes.bfloat16)).reshape(k // 32, 32, n)
    amax = np.abs(w).max(1)
    byte = np.clip(np.where(amax > 0, np.frexp(amax)[1] - 1 + 127 - 7, 1), 1, 254)
    scaled = (w * np.exp2(127.0 - byte)[:, None, :]).reshape(k, n).astype(np.float32)
    words = np.ascontiguousarray(scaled.reshape(k // 512, 128, 4, n).transpose(0, 1, 3, 2)).astype(ml_dtypes.float8_e4m3fn).view(np.uint8)
    return words, np.ascontiguousarray(byte.astype(np.uint8).reshape(k // 512, 16, n))


def unpack_weight(words, scales):
    g, p, n, _ = words.shape
    vals = np.ascontiguousarray(words).view(ml_dtypes.float8_e4m3fn).astype(np.float64) * np.repeat(np.exp2(scales.astype(np.float64) - 127.0), 8, axis=1)[..., None]
    return vals.transpose(0, 1, 3, 2).reshape(g * 512, n)


def planes(y):
    n, m = y.shape
    v = y.astype(np.float32).astype(ml_dtypes.bfloat16).astype(np.float64).reshape(n // 32, 32, m)
    top = np.abs(v).max(1)
    byte = np.clip(np.where(top > 0, np.frexp(top)[1] - 1 + 127 - 7, 1), 1, 254)
    codes = (v * np.exp2(127.0 - byte)[:, None, :]).reshape(n, m).astype(np.float32).astype(ml_dtypes.float8_e4m3fn).view(np.uint8)
    words = codes.reshape(n // 512, 128, 4, m).transpose(0, 1, 3, 2)
    return np.ascontiguousarray(words), np.ascontiguousarray(byte.astype(np.uint8).reshape(n // 512, 16, m))


def sigmoid(v):
    return 1.0 / (1.0 + np.exp(-np.maximum(v, -700.0)))


def silu(v):
    return v / (1.0 + np.exp(-np.maximum(v, -700.0)))


K, T, S, H, N = 1024, 2048, 512, 512, 512


def setup_inputs():
    n = np.random.standard_normal
    s = mx_kscale(K)[:, None]
    u = mx_kscale(H)
    packed_xT = pack_weight(n((K, T)) * s)
    return {
        "x_words": packed_xT[0],
        "x_scales": packed_xT[1],
        "w1": (n((K, N)) / np.sqrt(2 * K) / s).astype(np.float32),
        "w2": (n((K, N)) / np.sqrt(2 * K) / s).astype(np.float32),
        "w3": (n((K, H)) / np.sqrt(2 * K) / s * u).astype(np.float32),
        "w4": (n((K, H)) / np.sqrt(2 * K) / s * u).astype(np.float32),
        "w5": (n((H, N)) / np.sqrt(H) / u[:, None]).astype(np.float32),
        "offs": striped(np.random.permutation(T)[:S]),
        "prev": striped(np.random.permutation(T)[:S]),
    }


def reference(x_words, x_scales, w1, w2, w3, w4, w5, offs, prev):
    xq = unpack_weight(x_words, x_scales)[:, unstriped(offs)]
    x_prev = unpack_weight(x_words, x_scales)[:, unstriped(prev)]
    h = silu(mxq(f64(w3), 0, "e4m3").T @ xq + mxq(f64(w4), 0, "e4m3").T @ x_prev)
    y = mxq(f64(w5), 0, "e4m3").T @ mxq(h, 0, "e4m3")
    r = sigmoid(mxq(f64(w1), 0, "e4m3").T @ xq + mxq(f64(w2), 0, "e4m3").T @ x_prev)
    out_0 = y * r
    return (out_0,) + planes(out_0)

@@ -1,0 +1,208 @@
+from contextlib import ExitStack
+
+import concourse.mybir as mybir
+
+K, T, S, H, N = 1024, 2048, 512, 512, 512
+FLOPS = 2 * S * (2 * K * H + 2 * K * N + H * N)
+
+F32 = mybir.dt.float32
+BF16 = mybir.dt.bfloat16
+I32 = mybir.dt.int32
+U32 = mybir.dt.uint32
+U16 = mybir.dt.uint16
+U8 = mybir.dt.uint8
+FP8X4 = mybir.dt.float8_e4m3fn_x4
+ACT = mybir.ActivationFunctionType
+
+P = 128
+PACK = 4
+K_PASS = P * PACK
+PASSES = K // K_PASS
+CHUNK = 128
+CHUNKS = S // CHUNK
+QUADRANTS = 4
+SCALE_ROWS = 4
+
+
+def tile_picked_zshift_silu_po_kernel(
+    tc, x_words, x_scales, w1, w2, w3, w4, w5, offs, prev, out_0, out_1, out_2
+):
+    nc = tc.nc
+    with ExitStack() as ctx:
+        keep = ctx.enter_context(tc.tile_pool(name="keep", bufs=1))
+        psum = ctx.enter_context(tc.psum_pool(name="psum", bufs=1))
+
+        def load_words(g):
+            tile = keep.tile([P, T], U32, name="table_words%d" % g, align_bytes=64)
+            nc.sync.dma_start(tile[:].bitcast(I32), x_words[g].rearrange("p n t -> p (n t)").bitcast(I32))
+            return tile
+
+        table_words = [load_words(0)]
+        lists = []
+        for name, src in (("offs", offs), ("prev", prev)):
+            tile = keep.tile([P, S // 16], U16, name="list_" + name)
+            nc.sync.dma_start(tile[:], src)
+            lists.append(tile)
+
+        table_scales = keep.tile([P, T], U8, name="table_scales", align_bytes=64)
+        nc.vector.memset(table_scales[:].bitcast(I32), 0)
+        for q in range(QUADRANTS):
+            nc.sync.dma_start(
+                table_scales[32 * q : 32 * q + PASSES * SCALE_ROWS, :].bitcast(I32),
+                x_scales[:, SCALE_ROWS * q : SCALE_ROWS * (q + 1), :].bitcast(I32),
+            )
+        table_words.append(load_words(1))
+
+        raw = {}
+        for name, w in (("w3", w3), ("w4", w4), ("w1", w1), ("w2", w2)):
+            for g in range(PASSES):
+                tile = keep.tile([P, PACK, N], F32, name="raw_%s_%d" % (name, g), align_bytes=64)
+                nc.sync.dma_start(tile[:], w[g * K_PASS : (g + 1) * K_PASS, :].rearrange("(p j) c -> p j c", j=PACK))
+                raw[name, g] = tile
+        raw_w5 = []
+        for u in range(2):
+            tile = keep.tile([P, PACK, N // 2], F32, name="raw_w5_%d" % u, align_bytes=64)
+            nc.sync.dma_start(tile[:], w5[:, u * N // 2 : (u + 1) * N // 2].rearrange("(p j) c -> p j c", j=PACK))
+            raw_w5.append(tile)
+
+        picked_words = {}
+        picked_scales = []
+        for g in range(PASSES):
+            for side in range(2):
+                tile = keep.tile([P, S], U32, name="picked_words%d_%d" % (side, g), align_bytes=64)
+                nc.vector.tensor_copy(tile[:], table_words[g][:].indirect(lists[side][:]))
+                picked_words[side, g] = tile
+            tile = keep.tile([P, S], U8, name="picked_scales%d" % g, align_bytes=64)
+            nc.vector.tensor_copy(tile[:], table_scales[:].indirect(lists[g][:]))
+            picked_scales.append(tile)
+
+        def quantize_weight(name, g, scalar_share):
+            rounded = keep.tile([P, PACK * N], BF16, name="rounded_%s_%d" % (name, g), align_bytes=64)
+            dst = rounded[:].rearrange("p (t m j) -> p m j t", t=PACK, j=PACK)
+            src = raw[name, g][:].rearrange("p j (m t) -> p m j t", t=PACK)
+            cut = P - scalar_share
+            if cut > 0:
+                nc.vector.tensor_copy(dst[:, :cut], src[:, :cut])
+            if scalar_share > 0:
+                nc.scalar.copy(dst[:, cut:], src[:, cut:])
+            codes = keep.tile([P, N], U32, name="codes_%s_%d" % (name, g), align_bytes=64)
+            scales = keep.tile([P, N], U8, name="scales_%s_%d" % (name, g), align_bytes=64)
+            nc.vector.quantize_mx(out=codes[:].bitcast(FP8X4), scales=scales[:], in_=rounded[:])
+            return codes, scales
+
+        def two_token_product(banks, names, shares):
+            steps = [(side, g) for side in range(2) for g in range(PASSES)]
+            for n, (side, g) in enumerate(steps):
+                codes, scales = quantize_weight(names[side], g, shares[n])
+                last = n == len(steps) - 1
+                if last:
+                    order = [(t, c) for c in range(CHUNKS) for t in range(PACK)]
+                else:
+                    order = [(t, c) for t in range(PACK) for c in range(CHUNKS)]
+                for t, c in order:
+                    rows = slice(t * P, (t + 1) * P)
+                    cols = slice(c * CHUNK, (c + 1) * CHUNK)
+                    nc.tensor.matmul_mx(
+                        out=banks[c][:, t * CHUNK : (t + 1) * CHUNK],
+                        lhsT=codes[:, rows].bitcast(FP8X4),
+                        lhsT_scale=scales[:, rows],
+                        rhs=picked_words[side, g][:, cols].bitcast(FP8X4),
+                        rhs_scale=picked_scales[side][SCALE_ROWS * g :, cols],
+                        start=(n == 0 and t == 0),
+                        stop=(last and t == PACK - 1),
+                    )
+
+        h_banks = [psum.tile([P, PACK * CHUNK], F32, name="h_bank%d" % c, tag="hy%d" % c) for c in range(CHUNKS)]
+        two_token_product(h_banks, ("w3", "w4"), (64, 64, 64, 48))
+        h_rounded = keep.tile([P, PACK * S], BF16, name="h_rounded", align_bytes=64)
+        for c in range(CHUNKS):
+            h_sum = h_banks[c][:].rearrange("p (t n) -> p n t", t=PACK)
+            h_gate = keep.tile([P, CHUNK, PACK], F32, name="h_gate%d" % c, align_bytes=64)
+            nc.scalar.activation(h_gate[:], h_sum, ACT.Sigmoid)
+            nc.vector.tensor_tensor(
+                h_rounded[:, c * PACK * CHUNK : (c + 1) * PACK * CHUNK].rearrange("p (n t) -> p n t", t=PACK),
+                h_sum,
+                h_gate[:],
+                mybir.AluOpType.mult,
+            )
+
+        r_banks = [psum.tile([P, PACK * CHUNK], F32, name="r_bank%d" % c) for c in range(CHUNKS)]
+        two_token_product(r_banks, ("w1", "w2"), (48, 64, 64, 64))
+
+        h_codes = keep.tile([P, S], U32, name="h_codes", align_bytes=64)
+        h_scales = keep.tile([P, S], U8, name="h_scales", align_bytes=64)
+        nc.vector.quantize_mx(out=h_codes[:].bitcast(FP8X4), scales=h_scales[:], in_=h_rounded[:])
+
+        w5_codes = keep.tile([P, N], U32, name="w5_codes", align_bytes=64)
+        w5_scales = keep.tile([P, N], U8, name="w5_scales", align_bytes=64)
+        half = P // 2
+        w5_rounded = []
+        for u in range(2):
+            tile = keep.tile([P, PACK, half * PACK], BF16, name="rounded_w5_%d" % u, align_bytes=64)
+            dst = tile[:].rearrange("p t (m j) -> p m j t", j=PACK)
+            src = raw_w5[u][:].rearrange("p j (m t) -> p m j t", t=PACK)
+            if u == 0:
+                nc.scalar.copy(dst, src)
+            else:
+                nc.vector.tensor_copy(dst, src)
+            w5_rounded.append(tile)
+        for u in range(2):
+            for t in range(PACK):
+                cols = slice(t * P + u * half, t * P + (u + 1) * half)
+                nc.vector.quantize_mx(
+                    out=w5_codes[:, cols].bitcast(FP8X4), scales=w5_scales[:, cols], in_=w5_rounded[u][:, t, :]
+                )
+
+        gates = []
+        for c in range(CHUNKS):
+            tile = keep.tile([P, PACK, CHUNK], F32, name="gate%d" % c, align_bytes=64)
+            nc.scalar.activation(tile[:], r_banks[c][:].rearrange("p (t n) -> p t n", t=PACK), ACT.Sigmoid)
+            gates.append(tile)
+
+        out_codes = keep.tile([P, S], U32, name="out_codes", align_bytes=64)
+        out_scales = keep.tile([P, S], U8, name="out_scales", align_bytes=64)
+        out_rows = out_0.rearrange("(p t) n -> p t n", t=PACK)
+        words_rows = out_1[0].rearrange("p n t -> p (n t)").bitcast(I32)
+        results = []
+
+        def multiply(c):
+            cols = slice(c * CHUNK, (c + 1) * CHUNK)
+            y_bank = psum.tile([P, PACK * CHUNK], F32, name="y_bank%d" % c, tag="hy%d" % c)
+            for t in range(PACK):
+                rows = slice(t * P, (t + 1) * P)
+                nc.tensor.matmul_mx(
+                    out=y_bank[:, t * CHUNK : (t + 1) * CHUNK],
+                    lhsT=w5_codes[:, rows].bitcast(FP8X4),
+                    lhsT_scale=w5_scales[:, rows],
+                    rhs=h_codes[:, cols].bitcast(FP8X4),
+                    rhs_scale=h_scales[:, cols],
+                    start=True,
+                    stop=True,
+                )
+            result = keep.tile([P, PACK, CHUNK], F32, name="result%d" % c, align_bytes=64)
+            nc.vector.tensor_tensor(
+                result[:], y_bank[:].rearrange("p (t n) -> p t n", t=PACK), gates[c][:], mybir.AluOpType.mult
+            )
+            nc.sync.dma_start(out_rows[:, :, cols], result[:])
+            rounded = keep.tile([P, PACK * CHUNK], BF16, name="out_rounded%d" % c, align_bytes=64)
+            nc.scalar.copy(
+                rounded[:].rearrange("p (a i t) -> p a t i", i=4, t=PACK),
+                result[:].rearrange("p t (a i) -> p a t i", i=4),
+            )
+            results.append(rounded)
+
+        def quantize_out(c):
+            cols = slice(c * CHUNK, (c + 1) * CHUNK)
+            nc.vector.quantize_mx(out=out_codes[:, cols].bitcast(FP8X4), scales=out_scales[:, cols], in_=results[c][:])
+
+        for c in range(CHUNKS + 1):
+            if c < CHUNKS:
+                multiply(c)
+            if c > 0:
+                quantize_out(c - 1)
+        nc.sync.dma_start(words_rows, out_codes[:].bitcast(I32))
+        for q in range(QUADRANTS):
+            (nc.sync if q == QUADRANTS - 1 else nc.scalar).dma_start(
+                out_2[0, SCALE_ROWS * q : SCALE_ROWS * (q + 1), :].bitcast(I32),
+                out_scales[32 * q : 32 * q + SCALE_ROWS, :].bitcast(I32),
+            )

@@ -20,6 +20,8 @@ K_PASS = P * PACK
 PASSES = K // K_PASS
 CHUNK = 128
 CHUNKS = S // CHUNK
+HALF = S // 2
+BANK = 512
 QUADRANTS = 4
 SCALE_ROWS = 4
 
@@ -32,12 +34,6 @@ def tile_picked_zshift_silu_po_kernel(
         keep = ctx.enter_context(tc.tile_pool(name="keep", bufs=1))
         psum = ctx.enter_context(tc.psum_pool(name="psum", bufs=1))
 
-        def load_words(g):
-            tile = keep.tile([P, T], U32, name="table_words%d" % g, align_bytes=64)
-            nc.sync.dma_start(tile[:].bitcast(I32), x_words[g].rearrange("p n t -> p (n t)").bitcast(I32))
-            return tile
-
-        table_words = [load_words(0)]
         lists = []
         for name, src in (("offs", offs), ("prev", prev)):
             tile = keep.tile([P, S // 16], U16, name="list_" + name)
@@ -51,156 +47,152 @@ def tile_picked_zshift_silu_po_kernel(
                 table_scales[32 * q : 32 * q + PASSES * SCALE_ROWS, :].bitcast(I32),
                 x_scales[:, SCALE_ROWS * q : SCALE_ROWS * (q + 1), :].bitcast(I32),
             )
-        table_words.append(load_words(1))
 
         raw = {}
-        for name, w in (("w3", w3), ("w4", w4), ("w1", w1), ("w2", w2)):
-            for g in range(PASSES):
-                tile = keep.tile([P, PACK, N], F32, name="raw_%s_%d" % (name, g), align_bytes=64)
-                nc.sync.dma_start(tile[:], w[g * K_PASS : (g + 1) * K_PASS, :].rearrange("(p j) c -> p j c", j=PACK))
-                raw[name, g] = tile
-        raw_w5 = []
-        for u in range(2):
-            tile = keep.tile([P, PACK, N // 2], F32, name="raw_w5_%d" % u, align_bytes=64)
-            nc.sync.dma_start(tile[:], w5[:, u * N // 2 : (u + 1) * N // 2].rearrange("(p j) c -> p j c", j=PACK))
-            raw_w5.append(tile)
+        table_words = []
 
-        picked_words = {}
+        def load_weight(name, w, g):
+            tile = keep.tile([P, PACK, N], F32, name="raw_%s_%d" % (name, g), align_bytes=64)
+            nc.sync.dma_start(tile[:], w[g * K_PASS : (g + 1) * K_PASS, :].rearrange("(p j) c -> p j c", j=PACK))
+            raw[name, g] = tile
+
+        for g in range(PASSES):
+            load_weight("w3", w3, g)
+            tile = keep.tile([P, T], U32, name="table_words%d" % g, align_bytes=64)
+            nc.sync.dma_start(tile[:].bitcast(I32), x_words[g].rearrange("p n t -> p (n t)").bitcast(I32))
+            table_words.append(tile)
+        for name, w in (("w4", w4), ("w1", w1), ("w2", w2), ("w5", w5)):
+            for g in range(w.shape[0] // K_PASS):
+                load_weight(name, w, g)
+
         picked_scales = []
+        for side in range(2):
+            tile = keep.tile([P, S], U8, name="picked_scales%d" % side, align_bytes=64)
+            nc.vector.tensor_copy(tile[:], table_scales[:].indirect(lists[side][:]))
+            picked_scales.append(tile)
+        picked_words = {}
         for g in range(PASSES):
             for side in range(2):
                 tile = keep.tile([P, S], U32, name="picked_words%d_%d" % (side, g), align_bytes=64)
                 nc.vector.tensor_copy(tile[:], table_words[g][:].indirect(lists[side][:]))
                 picked_words[side, g] = tile
-            tile = keep.tile([P, S], U8, name="picked_scales%d" % g, align_bytes=64)
-            nc.vector.tensor_copy(tile[:], table_scales[:].indirect(lists[g][:]))
-            picked_scales.append(tile)
 
-        def quantize_weight(name, g, scalar_share):
-            rounded = keep.tile([P, PACK * N], BF16, name="rounded_%s_%d" % (name, g), align_bytes=64)
-            dst = rounded[:].rearrange("p (t m j) -> p m j t", t=PACK, j=PACK)
+        def quantize_weight(name, g, engines):
             src = raw[name, g][:].rearrange("p j (m t) -> p m j t", t=PACK)
-            cut = P - scalar_share
-            if cut > 0:
-                nc.vector.tensor_copy(dst[:, :cut], src[:, :cut])
-            if scalar_share > 0:
-                nc.scalar.copy(dst[:, cut:], src[:, cut:])
+            rounded = []
+            for pair in range(2):
+                tile = keep.tile([P, 2 * P * PACK], BF16, name="rounded_%s_%d_%d" % (name, g, pair), align_bytes=64)
+                engines[pair](tile[:].rearrange("p (e m j) -> p m j e", e=2, j=PACK), src[:, :, :, 2 * pair : 2 * pair + 2])
+                rounded.append(tile)
             codes = keep.tile([P, N], U32, name="codes_%s_%d" % (name, g), align_bytes=64)
             scales = keep.tile([P, N], U8, name="scales_%s_%d" % (name, g), align_bytes=64)
-            nc.vector.quantize_mx(out=codes[:].bitcast(FP8X4), scales=scales[:], in_=rounded[:])
+            for pair in range(2):
+                cols = slice(2 * pair * P, 2 * (pair + 1) * P)
+                nc.vector.quantize_mx(out=codes[:, cols].bitcast(FP8X4), scales=scales[:, cols], in_=rounded[pair][:])
             return codes, scales
 
-        def two_token_product(banks, names, shares):
+        on_scalar = (nc.scalar.copy, nc.scalar.copy)
+        on_vector = (nc.vector.tensor_copy, nc.vector.tensor_copy)
+        shared = (nc.vector.tensor_copy, nc.scalar.copy)
+
+        def two_token_product(place, width, names, shares):
             steps = [(side, g) for side in range(2) for g in range(PASSES)]
+            spans = range(S // width)
+            per_bank = BANK // width
             for n, (side, g) in enumerate(steps):
                 codes, scales = quantize_weight(names[side], g, shares[n])
                 last = n == len(steps) - 1
                 if last:
-                    order = [(t, c) for c in range(CHUNKS) for t in range(PACK)]
+                    order = [(t, c) for c in spans for t in range(PACK)]
                 else:
-                    order = [(t, c) for t in range(PACK) for c in range(CHUNKS)]
+                    order = [(t, c) for t in range(PACK) for c in spans]
                 for t, c in order:
                     rows = slice(t * P, (t + 1) * P)
-                    cols = slice(c * CHUNK, (c + 1) * CHUNK)
+                    cols = slice(c * width, (c + 1) * width)
                     nc.tensor.matmul_mx(
-                        out=banks[c][:, t * CHUNK : (t + 1) * CHUNK],
+                        out=place(t, c),
                         lhsT=codes[:, rows].bitcast(FP8X4),
                         lhsT_scale=scales[:, rows],
                         rhs=picked_words[side, g][:, cols].bitcast(FP8X4),
                         rhs_scale=picked_scales[side][SCALE_ROWS * g :, cols],
-                        start=(n == 0 and t == 0),
-                        stop=(last and t == PACK - 1),
+                        start=(n == 0 and t % per_bank == 0),
+                        stop=(last and t % per_bank == per_bank - 1),
                     )
 
         h_banks = [psum.tile([P, PACK * CHUNK], F32, name="h_bank%d" % c, tag="hy%d" % c) for c in range(CHUNKS)]
-        two_token_product(h_banks, ("w3", "w4"), (64, 64, 64, 48))
+        two_token_product(lambda t, c: h_banks[c][:, t * CHUNK : (t + 1) * CHUNK], CHUNK, ("w3", "w4"), (on_scalar, on_scalar, shared, shared))
         h_rounded = keep.tile([P, PACK * S], BF16, name="h_rounded", align_bytes=64)
         for c in range(CHUNKS):
-            h_sum = h_banks[c][:].rearrange("p (t n) -> p n t", t=PACK)
-            h_gate = keep.tile([P, CHUNK, PACK], F32, name="h_gate%d" % c, align_bytes=64)
-            nc.scalar.activation(h_gate[:], h_sum, ACT.Sigmoid)
-            nc.vector.tensor_tensor(
+            nc.scalar.activation(
                 h_rounded[:, c * PACK * CHUNK : (c + 1) * PACK * CHUNK].rearrange("p (n t) -> p n t", t=PACK),
-                h_sum,
-                h_gate[:],
-                mybir.AluOpType.mult,
+                h_banks[c][:].rearrange("p (t n) -> p n t", t=PACK),
+                ACT.Silu,
             )
 
         r_banks = [psum.tile([P, PACK * CHUNK], F32, name="r_bank%d" % c) for c in range(CHUNKS)]
-        two_token_product(r_banks, ("w1", "w2"), (48, 64, 64, 64))
+        two_token_product(
+            lambda t, u: r_banks[2 * u + t // 2][:, (t % 2) * HALF : (t % 2 + 1) * HALF], HALF, ("w1", "w2"), (on_vector, shared, shared, shared)
+        )
 
         h_codes = keep.tile([P, S], U32, name="h_codes", align_bytes=64)
         h_scales = keep.tile([P, S], U8, name="h_scales", align_bytes=64)
         nc.vector.quantize_mx(out=h_codes[:].bitcast(FP8X4), scales=h_scales[:], in_=h_rounded[:])
 
-        w5_codes = keep.tile([P, N], U32, name="w5_codes", align_bytes=64)
-        w5_scales = keep.tile([P, N], U8, name="w5_scales", align_bytes=64)
-        half = P // 2
-        w5_rounded = []
-        for u in range(2):
-            tile = keep.tile([P, PACK, half * PACK], BF16, name="rounded_w5_%d" % u, align_bytes=64)
-            dst = tile[:].rearrange("p t (m j) -> p m j t", j=PACK)
-            src = raw_w5[u][:].rearrange("p j (m t) -> p m j t", t=PACK)
-            if u == 0:
-                nc.scalar.copy(dst, src)
-            else:
-                nc.vector.tensor_copy(dst, src)
-            w5_rounded.append(tile)
-        for u in range(2):
-            for t in range(PACK):
-                cols = slice(t * P + u * half, t * P + (u + 1) * half)
-                nc.vector.quantize_mx(
-                    out=w5_codes[:, cols].bitcast(FP8X4), scales=w5_scales[:, cols], in_=w5_rounded[u][:, t, :]
-                )
+        w5_codes, w5_scales = quantize_weight("w5", 0, on_vector)
 
         gates = []
-        for c in range(CHUNKS):
-            tile = keep.tile([P, PACK, CHUNK], F32, name="gate%d" % c, align_bytes=64)
-            nc.scalar.activation(tile[:], r_banks[c][:].rearrange("p (t n) -> p t n", t=PACK), ACT.Sigmoid)
+        for b in range(4):
+            tile = keep.tile([P, BANK], F32, name="gate%d" % b, align_bytes=64)
+            nc.scalar.activation(tile[:], r_banks[b][:], ACT.Sigmoid)
             gates.append(tile)
 
         out_codes = keep.tile([P, S], U32, name="out_codes", align_bytes=64)
         out_scales = keep.tile([P, S], U8, name="out_scales", align_bytes=64)
         out_rows = out_0.rearrange("(p t) n -> p t n", t=PACK)
-        words_rows = out_1[0].rearrange("p n t -> p (n t)").bitcast(I32)
+        rounded = keep.tile([P, PACK * S], BF16, name="out_rounded", align_bytes=64)
         results = []
-
-        def multiply(c):
-            cols = slice(c * CHUNK, (c + 1) * CHUNK)
-            y_bank = psum.tile([P, PACK * CHUNK], F32, name="y_bank%d" % c, tag="hy%d" % c)
-            for t in range(PACK):
-                rows = slice(t * P, (t + 1) * P)
-                nc.tensor.matmul_mx(
-                    out=y_bank[:, t * CHUNK : (t + 1) * CHUNK],
-                    lhsT=w5_codes[:, rows].bitcast(FP8X4),
-                    lhsT_scale=w5_scales[:, rows],
-                    rhs=h_codes[:, cols].bitcast(FP8X4),
-                    rhs_scale=h_scales[:, cols],
-                    start=True,
-                    stop=True,
+        for u in range(2):
+            cols = slice(u * HALF, (u + 1) * HALF)
+            result = keep.tile([P, PACK, HALF], F32, name="result%d" % u, align_bytes=64)
+            results.append(result)
+            for pair in range(2):
+                b = 2 * u + pair
+                y_bank = psum.tile([P, BANK], F32, name="y_bank%d" % b, tag="hy%d" % b)
+                for e in range(2):
+                    t = 2 * pair + e
+                    rows = slice(t * P, (t + 1) * P)
+                    nc.tensor.matmul_mx(
+                        out=y_bank[:, e * HALF : (e + 1) * HALF],
+                        lhsT=w5_codes[:, rows].bitcast(FP8X4),
+                        lhsT_scale=w5_scales[:, rows],
+                        rhs=h_codes[:, cols].bitcast(FP8X4),
+                        rhs_scale=h_scales[:, cols],
+                        start=True,
+                        stop=True,
+                    )
+                piece = result[:, 2 * pair : 2 * pair + 2, :]
+                nc.vector.tensor_tensor(
+                    piece.rearrange("p t n -> p (t n)"), y_bank[:], gates[b][:], mybir.AluOpType.mult
                 )
-            result = keep.tile([P, PACK, CHUNK], F32, name="result%d" % c, align_bytes=64)
-            nc.vector.tensor_tensor(
-                result[:], y_bank[:].rearrange("p (t n) -> p t n", t=PACK), gates[c][:], mybir.AluOpType.mult
-            )
-            nc.sync.dma_start(out_rows[:, :, cols], result[:])
-            rounded = keep.tile([P, PACK * CHUNK], BF16, name="out_rounded%d" % c, align_bytes=64)
-            nc.scalar.copy(
-                rounded[:].rearrange("p (a i t) -> p a t i", i=4, t=PACK),
-                result[:].rearrange("p t (a i) -> p a t i", i=4),
-            )
-            results.append(rounded)
+                nc.sync.dma_start(out_rows[:, 2 * pair : 2 * pair + 2, cols], piece)
 
-        def quantize_out(c):
-            cols = slice(c * CHUNK, (c + 1) * CHUNK)
-            nc.vector.quantize_mx(out=out_codes[:, cols].bitcast(FP8X4), scales=out_scales[:, cols], in_=results[c][:])
+        def round_out(engine_copy, c):
+            u, n0 = divmod(c * CHUNK, HALF)
+            engine_copy(
+                rounded[:, c * PACK * CHUNK : (c + 1) * PACK * CHUNK].rearrange("p (a i t) -> p a t i", i=4, t=PACK),
+                results[u][:, :, n0 : n0 + CHUNK].rearrange("p t (a i) -> p a t i", i=4),
+            )
 
-        for c in range(CHUNKS + 1):
-            if c < CHUNKS:
-                multiply(c)
-            if c > 0:
-                quantize_out(c - 1)
-        nc.sync.dma_start(words_rows, out_codes[:].bitcast(I32))
+        for c in range(CHUNKS):
+            round_out(nc.vector.tensor_copy if c == CHUNKS - 1 else nc.scalar.copy, c)
+        for u in range(2):
+            cols = slice(u * HALF, (u + 1) * HALF)
+            nc.vector.quantize_mx(
+                out=out_codes[:, cols].bitcast(FP8X4),
+                scales=out_scales[:, cols],
+                in_=rounded[:, u * PACK * HALF : (u + 1) * PACK * HALF],
+            )
+        nc.sync.dma_start(out_1[0].rearrange("p n t -> p (n t)").bitcast(I32), out_codes[:].bitcast(I32))
         for q in range(QUADRANTS):
             (nc.sync if q == QUADRANTS - 1 else nc.scalar).dma_start(
                 out_2[0, SCALE_ROWS * q : SCALE_ROWS * (q + 1), :].bitcast(I32),

@@ -34,6 +34,15 @@ def tile_picked_zshift_silu_po_kernel(
         keep = ctx.enter_context(tc.tile_pool(name="keep", bufs=1))
         psum = ctx.enter_context(tc.psum_pool(name="psum", bufs=1))
 
+        raw = {}
+        table_words = []
+
+        def load_weight(name, w, g):
+            tile = keep.tile([P, PACK, N], F32, name="raw_%s_%d" % (name, g), align_bytes=64)
+            nc.sync.dma_start(tile[:], w[g * K_PASS : (g + 1) * K_PASS, :].rearrange("(p j) c -> p j c", j=PACK))
+            raw[name, g] = tile
+
+        load_weight("w3", w3, 0)
         lists = []
         for name, src in (("offs", offs), ("prev", prev)):
             tile = keep.tile([P, S // 16], U16, name="list_" + name)
@@ -48,16 +57,9 @@ def tile_picked_zshift_silu_po_kernel(
                 x_scales[:, SCALE_ROWS * q : SCALE_ROWS * (q + 1), :].bitcast(I32),
             )
 
-        raw = {}
-        table_words = []
-
-        def load_weight(name, w, g):
-            tile = keep.tile([P, PACK, N], F32, name="raw_%s_%d" % (name, g), align_bytes=64)
-            nc.sync.dma_start(tile[:], w[g * K_PASS : (g + 1) * K_PASS, :].rearrange("(p j) c -> p j c", j=PACK))
-            raw[name, g] = tile
-
         for g in range(PASSES):
-            load_weight("w3", w3, g)
+            if g > 0:
+                load_weight("w3", w3, g)
             tile = keep.tile([P, T], U32, name="table_words%d" % g, align_bytes=64)
             nc.sync.dma_start(tile[:].bitcast(I32), x_words[g].rearrange("p n t -> p (n t)").bitcast(I32))
             table_words.append(tile)

from contextlib import ExitStack

import concourse.mybir as mybir

K, T, S, H, N = 1024, 2048, 512, 512, 512
FLOPS = 2 * S * (2 * K * H + 2 * K * N + H * N)

F32 = mybir.dt.float32
BF16 = mybir.dt.bfloat16
I32 = mybir.dt.int32
U32 = mybir.dt.uint32
U16 = mybir.dt.uint16
U8 = mybir.dt.uint8
FP8X4 = mybir.dt.float8_e4m3fn_x4
ACT = mybir.ActivationFunctionType

P = 128
PACK = 4
K_PASS = P * PACK
PASSES = K // K_PASS
CHUNK = 128
CHUNKS = S // CHUNK
HALF = S // 2
BANK = 512
QUADRANTS = 4
SCALE_ROWS = 4


def tile_picked_zshift_silu_po_kernel(
    tc, x_words, x_scales, w1, w2, w3, w4, w5, offs, prev, out_0, out_1, out_2
):
    nc = tc.nc
    with ExitStack() as ctx:
        keep = ctx.enter_context(tc.tile_pool(name="keep", bufs=1))
        psum = ctx.enter_context(tc.psum_pool(name="psum", bufs=1))

        raw = {}
        table_words = []

        def load_weight(name, w, g):
            tile = keep.tile([P, PACK, N], F32, name="raw_%s_%d" % (name, g), align_bytes=64)
            nc.sync.dma_start(tile[:], w[g * K_PASS : (g + 1) * K_PASS, :].rearrange("(p j) c -> p j c", j=PACK))
            raw[name, g] = tile

        load_weight("w3", w3, 0)
        lists = []
        for name, src in (("offs", offs), ("prev", prev)):
            tile = keep.tile([P, S // 16], U16, name="list_" + name)
            nc.sync.dma_start(tile[:], src)
            lists.append(tile)

        table_scales = keep.tile([P, T], U8, name="table_scales", align_bytes=64)
        nc.vector.memset(table_scales[:].bitcast(I32), 0)
        for q in range(QUADRANTS):
            nc.sync.dma_start(
                table_scales[32 * q : 32 * q + PASSES * SCALE_ROWS, :].bitcast(I32),
                x_scales[:, SCALE_ROWS * q : SCALE_ROWS * (q + 1), :].bitcast(I32),
            )

        for g in range(PASSES):
            if g > 0:
                load_weight("w3", w3, g)
            tile = keep.tile([P, T], U32, name="table_words%d" % g, align_bytes=64)
            nc.sync.dma_start(tile[:].bitcast(I32), x_words[g].rearrange("p n t -> p (n t)").bitcast(I32))
            table_words.append(tile)
        for name, w in (("w4", w4), ("w1", w1), ("w2", w2), ("w5", w5)):
            for g in range(w.shape[0] // K_PASS):
                load_weight(name, w, g)

        picked_scales = []
        for side in range(2):
            tile = keep.tile([P, S], U8, name="picked_scales%d" % side, align_bytes=64)
            nc.vector.tensor_copy(tile[:], table_scales[:].indirect(lists[side][:]))
            picked_scales.append(tile)
        picked_words = {}
        for g in range(PASSES):
            for side in range(2):
                tile = keep.tile([P, S], U32, name="picked_words%d_%d" % (side, g), align_bytes=64)
                nc.vector.tensor_copy(tile[:], table_words[g][:].indirect(lists[side][:]))
                picked_words[side, g] = tile

        def quantize_weight(name, g, engines):
            src = raw[name, g][:].rearrange("p j (m t) -> p m j t", t=PACK)
            rounded = []
            for pair in range(2):
                tile = keep.tile([P, 2 * P * PACK], BF16, name="rounded_%s_%d_%d" % (name, g, pair), align_bytes=64)
                engines[pair](tile[:].rearrange("p (e m j) -> p m j e", e=2, j=PACK), src[:, :, :, 2 * pair : 2 * pair + 2])
                rounded.append(tile)
            codes = keep.tile([P, N], U32, name="codes_%s_%d" % (name, g), align_bytes=64)
            scales = keep.tile([P, N], U8, name="scales_%s_%d" % (name, g), align_bytes=64)
            for pair in range(2):
                cols = slice(2 * pair * P, 2 * (pair + 1) * P)
                nc.vector.quantize_mx(out=codes[:, cols].bitcast(FP8X4), scales=scales[:, cols], in_=rounded[pair][:])
            return codes, scales

        on_scalar = (nc.scalar.copy, nc.scalar.copy)
        on_vector = (nc.vector.tensor_copy, nc.vector.tensor_copy)
        shared = (nc.vector.tensor_copy, nc.scalar.copy)

        def two_token_product(place, width, names, shares):
            steps = [(side, g) for side in range(2) for g in range(PASSES)]
            spans = range(S // width)
            per_bank = BANK // width
            for n, (side, g) in enumerate(steps):
                codes, scales = quantize_weight(names[side], g, shares[n])
                last = n == len(steps) - 1
                if last:
                    order = [(t, c) for c in spans for t in range(PACK)]
                else:
                    order = [(t, c) for t in range(PACK) for c in spans]
                for t, c in order:
                    rows = slice(t * P, (t + 1) * P)
                    cols = slice(c * width, (c + 1) * width)
                    nc.tensor.matmul_mx(
                        out=place(t, c),
                        lhsT=codes[:, rows].bitcast(FP8X4),
                        lhsT_scale=scales[:, rows],
                        rhs=picked_words[side, g][:, cols].bitcast(FP8X4),
                        rhs_scale=picked_scales[side][SCALE_ROWS * g :, cols],
                        start=(n == 0 and t % per_bank == 0),
                        stop=(last and t % per_bank == per_bank - 1),
                    )

        h_banks = [psum.tile([P, PACK * CHUNK], F32, name="h_bank%d" % c, tag="hy%d" % c) for c in range(CHUNKS)]
        two_token_product(lambda t, c: h_banks[c][:, t * CHUNK : (t + 1) * CHUNK], CHUNK, ("w3", "w4"), (on_scalar, on_scalar, shared, shared))
        h_rounded = keep.tile([P, PACK * S], BF16, name="h_rounded", align_bytes=64)
        for c in range(CHUNKS):
            nc.scalar.activation(
                h_rounded[:, c * PACK * CHUNK : (c + 1) * PACK * CHUNK].rearrange("p (n t) -> p n t", t=PACK),
                h_banks[c][:].rearrange("p (t n) -> p n t", t=PACK),
                ACT.Silu,
            )

        r_banks = [psum.tile([P, PACK * CHUNK], F32, name="r_bank%d" % c) for c in range(CHUNKS)]
        two_token_product(
            lambda t, u: r_banks[2 * u + t // 2][:, (t % 2) * HALF : (t % 2 + 1) * HALF], HALF, ("w1", "w2"), (on_vector, shared, shared, shared)
        )

        h_codes = keep.tile([P, S], U32, name="h_codes", align_bytes=64)
        h_scales = keep.tile([P, S], U8, name="h_scales", align_bytes=64)
        nc.vector.quantize_mx(out=h_codes[:].bitcast(FP8X4), scales=h_scales[:], in_=h_rounded[:])

        w5_codes, w5_scales = quantize_weight("w5", 0, on_vector)

        gates = []
        for b in range(4):
            tile = keep.tile([P, BANK], F32, name="gate%d" % b, align_bytes=64)
            nc.scalar.activation(tile[:], r_banks[b][:], ACT.Sigmoid)
            gates.append(tile)

        out_codes = keep.tile([P, S], U32, name="out_codes", align_bytes=64)
        out_scales = keep.tile([P, S], U8, name="out_scales", align_bytes=64)
        out_rows = out_0.rearrange("(p t) n -> p t n", t=PACK)
        rounded = keep.tile([P, PACK * S], BF16, name="out_rounded", align_bytes=64)
        results = []
        for u in range(2):
            cols = slice(u * HALF, (u + 1) * HALF)
            result = keep.tile([P, PACK, HALF], F32, name="result%d" % u, align_bytes=64)
            results.append(result)
            for pair in range(2):
                b = 2 * u + pair
                y_bank = psum.tile([P, BANK], F32, name="y_bank%d" % b, tag="hy%d" % b)
                for e in range(2):
                    t = 2 * pair + e
                    rows = slice(t * P, (t + 1) * P)
                    nc.tensor.matmul_mx(
                        out=y_bank[:, e * HALF : (e + 1) * HALF],
                        lhsT=w5_codes[:, rows].bitcast(FP8X4),
                        lhsT_scale=w5_scales[:, rows],
                        rhs=h_codes[:, cols].bitcast(FP8X4),
                        rhs_scale=h_scales[:, cols],
                        start=True,
                        stop=True,
                    )
                piece = result[:, 2 * pair : 2 * pair + 2, :]
                nc.vector.tensor_tensor(
                    piece.rearrange("p t n -> p (t n)"), y_bank[:], gates[b][:], mybir.AluOpType.mult
                )
                nc.sync.dma_start(out_rows[:, 2 * pair : 2 * pair + 2, cols], piece)

        def round_out(engine_copy, c):
            u, n0 = divmod(c * CHUNK, HALF)
            engine_copy(
                rounded[:, c * PACK * CHUNK : (c + 1) * PACK * CHUNK].rearrange("p (a i t) -> p a t i", i=4, t=PACK),
                results[u][:, :, n0 : n0 + CHUNK].rearrange("p t (a i) -> p a t i", i=4),
            )

        for c in range(CHUNKS):
            round_out(nc.vector.tensor_copy if c == CHUNKS - 1 else nc.scalar.copy, c)
        for u in range(2):
            cols = slice(u * HALF, (u + 1) * HALF)
            nc.vector.quantize_mx(
                out=out_codes[:, cols].bitcast(FP8X4),
                scales=out_scales[:, cols],
                in_=rounded[:, u * PACK * HALF : (u + 1) * PACK * HALF],
            )
        nc.sync.dma_start(out_1[0].rearrange("p n t -> p (n t)").bitcast(I32), out_codes[:].bitcast(I32))
        for q in range(QUADRANTS):
            (nc.sync if q == QUADRANTS - 1 else nc.scalar).dma_start(
                out_2[0, SCALE_ROWS * q : SCALE_ROWS * (q + 1), :].bitcast(I32),
                out_scales[32 * q : 32 * q + SCALE_ROWS, :].bitcast(I32),
            )
